import numpy as np
import ml_dtypes


def mxq(x, axis, fmt="e4m3"):
    dtype, down = {"e4m3": (ml_dtypes.float8_e4m3fn, 7), "e5m2": (ml_dtypes.float8_e5m2, 14)}[fmt]
    v = np.moveaxis(np.asarray(x, np.float32).astype(ml_dtypes.bfloat16).astype(np.float64), axis, -1)
    blocks = v.reshape(v.shape[:-1] + (-1, 32))
    amax = np.abs(blocks).max(-1, keepdims=True)
    byte = np.maximum(np.where(amax > 0, np.frexp(amax)[1] - 1 + 127, 0) - down, 1)
    scale = np.exp2(byte - 127.0)
    codes = (blocks / scale).astype(np.float32).astype(dtype).astype(np.float64)
    return np.moveaxis((codes * scale).reshape(v.shape), -1, axis)


WIDE = False


def mx_kscale(k):
    if not WIDE:
        return np.ones(k)
    levels = np.array([10, -10, 5, -5, 0])
    if k % 512:
        return np.exp2(np.random.permutation(np.resize(levels, k // 32))).repeat(32)
    a = np.empty((k // 512, 16))
    for p in range(k // 512):
        a[p, :8] = np.random.permutation(np.resize(levels, 8))
        for g in range(8):
            far = levels[np.abs(levels - a[p, g]) >= 10]
            a[p, g + 8] = far[np.random.randint(len(far))]
    return np.exp2(a.ravel()).repeat(32)


def f64(x):
    return np.asarray(x).astype(np.float64)


def striped(idx):
    return np.tile(idx.reshape(-1, 16).T, (8, 1)).astype(np.uint16)


def unstriped(offs):
    return offs[:16].T.reshape(-1).astype(np.int64)


E2M1 = np.array([0.0, 0.5, 1.0, 1.5, 2.0, 3.0, 4.0, 6.0, -0.0, -0.5, -1.0, -1.5, -2.0, -3.0, -4.0, -6.0])


def pack_weight(w, fmt):
    k, n = w.shape
    w = f64(np.asarray(w, np.float32).astype(ml_dtypes.bfloat16)).reshape(k // 32, 32, n)
    amax = np.abs(w).max(1)
    if fmt == "e4m3":
        byte = np.frexp(amax)[1] - 1 + 127 - 7
    else:
        mant, ex = np.frexp(amax / 6.0)
        byte = np.where(mant > 0.5, ex, ex - 1) + 127
    byte = np.clip(np.where(amax > 0, byte, 1), 1, 254)
    scaled = (w * np.exp2(127.0 - byte)[:, None, :]).reshape(k, n).astype(np.float32)
    by_word = np.ascontiguousarray(scaled.reshape(k // 512, 128, 4, n).transpose(0, 1, 3, 2))
    if fmt == "e4m3":
        words = by_word.astype(ml_dtypes.float8_e4m3fn).view(np.uint8)
    else:
        c = by_word.astype(ml_dtypes.float4_e2m1fn).view(np.uint8) & 0xF
        words = (c[..., 0::2] | (c[..., 1::2] << 4)).reshape(k // 512, 128, 2 * n)
    return np.ascontiguousarray(words), np.ascontiguousarray(byte.astype(np.uint8).reshape(k // 512, 16, n))


def unpack_weight(words, scales, fmt):
    g, _, n = scales.shape
    words = np.ascontiguousarray(words).reshape(g, 128, n, -1)
    if fmt == "e4m3":
        vals = words.view(ml_dtypes.float8_e4m3fn).astype(np.float64)
    else:
        nib = np.empty((g, 128, n, 4), np.uint8)
        nib[..., 0::2] = words & 0xF
        nib[..., 1::2] = words >> 4
        vals = E2M1[nib]
    vals = vals * np.repeat(np.exp2(scales.astype(np.float64) - 127.0), 8, axis=1)[..., None]
    return vals.transpose(0, 1, 3, 2).reshape(g * 512, n)


def gelu(v):
    return 0.5 * v * (1.0 + np.tanh(np.sqrt(2.0 / np.pi) * (v + 0.044715 * v**3)))


K, T, S, H, P, N = 1024, 4096, 1024, 1024, 512, 512


def setup_inputs():
    n = np.random.standard_normal
    s = mx_kscale(K)[:, None]
    u = mx_kscale(H)[:, None]
    d = {}
    d["tab_words"], d["tab_scales"] = pack_weight(n((K, T)) * s, "e2m1")
    d["offs"] = striped(np.random.permutation(T)[:S])
    d["w1"] = (0.54 * n((K, H)) / K ** 0.5 / s).astype(np.float32)
    d["gain"] = (2.0 * np.exp(0.3 * n(H)) * u[:, 0]).astype(np.float32)
    d["pos1"] = striped(np.random.permutation(S)[:P])
    d["pos2"] = striped(np.random.permutation(S)[:P])
    d["polish"] = (0.8 * n((H, P)) * u).astype(np.float32)
    d["w4_words"], d["w4_scales"] = pack_weight(1.1 * n((H, N)) / H ** 0.5 / u, "e2m1")
    return d


def reference(tab_words, tab_scales, offs, w1, gain, pos1, pos2, polish, w4_words, w4_scales):
    v = unpack_weight(tab_words, tab_scales, "e2m1")[:, unstriped(offs)]
    bands = np.sin(mxq(f64(w1), 0, "e4m3").T @ v)
    h = f64(gain)[:, None] * bands
    left = h[:, unstriped(pos1)] + f64(polish)
    z = np.maximum(left, h[:, unstriped(pos2)])
    w4 = unpack_weight(w4_words, w4_scales, "e2m1")
    y = w4.T @ mxq(z, 0, "e4m3")
    return np.tanh(y)

@@ -1,0 +1,276 @@
+import math
+from contextlib import ExitStack
+
+import concourse.mybir as mybir
+
+K, T, S, H, PAIRS, N = 1024, 4096, 1024, 1024, 512, 512
+FLOPS = 2 * K * H * S + 2 * H * N * PAIRS
+
+F32 = mybir.dt.float32
+BF16 = mybir.dt.bfloat16
+I32 = mybir.dt.int32
+U32 = mybir.dt.uint32
+U16 = mybir.dt.uint16
+U8 = mybir.dt.uint8
+FP8X4 = mybir.dt.float8_e4m3fn_x4
+FP4X4 = mybir.dt.float4_e2m1fn_x4
+ALU = mybir.AluOpType
+ACT = mybir.ActivationFunctionType
+
+P = 128
+PACK = 4
+PASS = P * PACK
+BANK = 512
+TWO_PI = 2.0 * math.pi
+TURN_OFFSET = 1024.0
+VECTOR_TURN_SLICES = (0, 1, 2)
+TEST_OFFSET = 1.0
+CHUNK = 128
+LATE_SHARE = 128
+SHIFT_BUFS = 2
+H_BUFS = 3
+SCALAR_SHARE = 48
+WEAVE_PIECES = 4
+
+
+def tile_list_slab_bookmatch_features_kernel(
+    tc, tab_words, tab_scales, offs, w1, gain, pos1, pos2, polish, w4_words, w4_scales, out
+):
+    nc = tc.nc
+    with ExitStack() as ctx:
+        keep = ctx.enter_context(tc.tile_pool(name="keep", bufs=1))
+        ring = ctx.enter_context(tc.tile_pool(name="ring", bufs=2))
+        psum = ctx.enter_context(tc.psum_pool(name="psum", bufs=8))
+
+        offs_sb = keep.tile([P, S // 16], U16, name="offs_sb")
+        pos1_sb = keep.tile([P, PAIRS // 16], U16, name="pos1_sb")
+        pos2_sb = keep.tile([P, PAIRS // 16], U16, name="pos2_sb")
+
+        scale_table = keep.tile([P, T], U8, name="scale_table", tag="slot6", align_bytes=64)
+        picked_scales = keep.tile([P, S], U8, name="picked_scales", align_bytes=64)
+        v_scales = [keep.tile([P, S], U8, name="v_scales%d" % a, align_bytes=64) for a in range(2)]
+        nc.vector.memset(scale_table[0:96, :].bitcast(I32), 0)
+        for a in range(2):
+            nc.vector.memset(v_scales[a][:].bitcast(I32), 0)
+
+        w_raw = {}
+
+        def load_w(a, b, tag):
+            raw = keep.tile([P, PACK, PASS], F32, name="w_raw%d%d" % (a, b), tag=tag, align_bytes=64)
+            rows = w1[a * PASS : (a + 1) * PASS, b * PASS : (b + 1) * PASS]
+            nc.sync.dma_start(out=raw[:], in_=rows.rearrange("(p i) c -> p i c", i=PACK))
+            w_raw[a, b] = raw
+
+        word_table = {}
+
+        def load_words(a, tag):
+            table = keep.tile([P, T], U16, name="word_table%d" % a, tag=tag, align_bytes=64)
+            nc.sync.dma_start(out=table[:].bitcast(I32), in_=tab_words[a].bitcast(I32))
+            word_table[a] = table
+
+        def move_scales(a):
+            for q in range(4):
+                row = 96 + 16 * a + 4 * q
+                nc.sync.dma_start(
+                    out=v_scales[a][32 * q : 32 * q + 4, :].bitcast(I32),
+                    in_=picked_scales[row : row + 4, :].bitcast(I32),
+                )
+
+        polish_sb = {}
+
+        def load_polish(b, tag):
+            pol = keep.tile([P, PACK, PAIRS], F32, name="polish%d" % b, tag=tag, align_bytes=64)
+            rows = polish[b * PASS : (b + 1) * PASS, :].rearrange("(p t) j -> p t j", t=PACK)
+            nc.sync.dma_start(out=pol[:], in_=rows)
+            polish_sb[b] = pol
+
+        nc.sync.dma_start(
+            out=scale_table[96:128, :].bitcast(I32),
+            in_=tab_scales.rearrange("a q t -> (a q) t").bitcast(I32),
+        )
+        nc.sync.dma_start(offs_sb[:], offs)
+        load_words(0, "slot7")
+        nc.sync.dma_start(pos1_sb[:], pos1)
+        nc.sync.dma_start(pos2_sb[:], pos2)
+        gain_sb = keep.tile([P, 2, PACK], F32, name="gain_sb")
+        nc.sync.dma_start(out=gain_sb[:], in_=gain.rearrange("(b p t) -> p b t", b=2, t=PACK))
+        load_w(0, 0, "slot0")
+        load_w(1, 0, "slot1")
+
+        w_codes, w_scales = {}, {}
+
+        w_grouped = {}
+
+        def weave_w(a, b, tag, m0, m1, engine_copy):
+            if (a, b) not in w_grouped:
+                w_grouped[a, b] = keep.tile(
+                    [P, PACK * PASS], BF16, name="w_grouped%d%d" % (a, b), tag=tag, align_bytes=64
+                )
+            engine_copy(
+                out=w_grouped[a, b][:].rearrange("p (t m i) -> p m i t", t=PACK, i=PACK)[:, m0:m1],
+                in_=w_raw[a, b][:].rearrange("p i (m t) -> p m i t", t=PACK)[:, m0:m1],
+            )
+
+        def quantise_w(a, b):
+            codes = keep.tile([P, PASS], U32, name="w_codes%d%d" % (a, b), align_bytes=64)
+            scales = keep.tile([P, PASS], U8, name="w_scales%d%d" % (a, b), align_bytes=64)
+            nc.vector.quantize_mx(out=codes[:].bitcast(FP8X4), scales=scales[:], in_=w_grouped[a, b][:])
+            w_codes[a, b], w_scales[a, b] = codes, scales
+
+        v_words = {}
+
+        def pick_words(a):
+            for u in range(2):
+                words = keep.tile([P, BANK], U16, name="v_words%d%d" % (a, u), align_bytes=64)
+                nc.vector.tensor_copy(words[:], word_table[a][:].indirect(offs_sb[:, 32 * u : 32 * u + 32]))
+                v_words[a, u] = words
+
+        nc.vector.tensor_copy(picked_scales[:], scale_table[:].indirect(offs_sb[:]))
+        move_scales(0)
+        load_words(1, "slot6")
+        move_scales(1)
+        pick_words(0)
+        for a in range(2):
+            weave_w(a, 0, "slot%d" % (2 + a), 0, SCALAR_SHARE, nc.scalar.copy)
+            weave_w(a, 0, "slot%d" % (2 + a), SCALAR_SHARE, P, nc.vector.tensor_copy)
+            quantise_w(a, 0)
+        pick_words(1)
+        load_w(0, 1, "slot0")
+        load_polish(0, "slot2")
+        load_w(1, 1, "slot1")
+        load_polish(1, "slot3")
+
+        left = [keep.tile([P, PACK, PAIRS], F32, name="left%d" % b) for b in range(2)]
+        right = [keep.tile([P, PACK, PAIRS], F32, name="right%d" % b) for b in range(2)]
+        z_codes = [keep.tile([P, PAIRS], U32, name="z_codes%d" % b, align_bytes=64) for b in range(2)]
+        z_scales = [keep.tile([P, PAIRS], U8, name="z_scales%d" % b, align_bytes=64) for b in range(2)]
+        z_bf = [keep.tile([P, PACK * PAIRS], BF16, name="z_bf%d" % b, align_bytes=64) for b in range(2)]
+
+        halves = [slice(u * BANK, (u + 1) * BANK) for u in range(2)]
+
+        def reduce_angle(b, t):
+            m_cols = slice(t * P, (t + 1) * P)
+            angle = ring.tile([P, S], F32, name="angle")
+            sums = []
+            for u, cols in enumerate(halves):
+                x = psum.tile([P, BANK], F32, name="x", tag="bank")
+                for a in range(2):
+                    nc.tensor.matmul_mx(
+                        out=x[:],
+                        lhsT=w_codes[a, b][:, m_cols].bitcast(FP8X4),
+                        lhsT_scale=w_scales[a, b][:, m_cols],
+                        rhs=v_words[a, u][:].bitcast(FP4X4),
+                        rhs_scale=v_scales[a][:, cols],
+                        start=(a == 0),
+                        stop=(a == 1),
+                    )
+                sums.append((x, cols))
+            if PACK * b + t in VECTOR_TURN_SLICES:
+                turns = ring.tile([P, S], I32, name="turns_i", bufs=1)
+                for x, cols in sums:
+                    nc.vector.tensor_scalar(turns[:, cols], x[:], 1.0 / TWO_PI, TEST_OFFSET, ALU.mult, ALU.add)
+                for x, cols in sums:
+                    nc.vector.scalar_tensor_tensor(angle[:, cols], turns[:, cols], -TWO_PI, x[:], ALU.mult, ALU.add)
+                return angle, TEST_OFFSET * TWO_PI
+            turns = ring.tile([P, S], U32, name="turns_u", bufs=1)
+            shift = ring.tile([P, S], F32, name="shift", bufs=SHIFT_BUFS)
+            for x, cols in sums:
+                nc.scalar.activation(turns[:, cols], x[:], ACT.Copy, bias=TURN_OFFSET, scale=1.0 / TWO_PI)
+            for x, cols in sums:
+                nc.scalar.activation(shift[:, cols], turns[:, cols], ACT.Copy, bias=TURN_OFFSET * TWO_PI, scale=-TWO_PI)
+            for x, cols in sums:
+                nc.vector.tensor_tensor(angle[:, cols], x[:], shift[:, cols], ALU.add)
+            return angle, 0.0
+
+        def make_h(b, t, angle, bias):
+            bands = ring.tile([P, S], F32, name="bands", bufs=1)
+            h = ring.tile([P, S], F32, name="h", bufs=H_BUFS)
+            for cols in halves:
+                nc.scalar.activation(bands[:, cols], angle[:, cols], ACT.Sin, bias=bias)
+            for cols in halves:
+                nc.scalar.activation(h[:, cols], bands[:, cols], ACT.Copy, scale=gain_sb[:, b, t : t + 1])
+            return h
+
+        def pick(b, t, h):
+            nc.vector.tensor_tensor(
+                left[b][:, t, :], h[:].indirect(pos1_sb[:]), polish_sb[b][:, t, :], ALU.add
+            )
+            nc.vector.tensor_copy(right[b][:, t, :], h[:].indirect(pos2_sb[:]))
+
+        def join(b, j0, j1):
+            nc.vector.tensor_tensor(
+                z_bf[b][:, PACK * j0 : PACK * j1].rearrange("p (c i t) -> p c t i", i=4, t=PACK),
+                left[b][:, :, j0:j1].rearrange("p t (c i) -> p c t i", i=4),
+                right[b][:, :, j0:j1].rearrange("p t (c i) -> p c t i", i=4),
+                ALU.max,
+            )
+
+        def quantise_z(b, j0, j1):
+            nc.vector.quantize_mx(
+                out=z_codes[b][:, j0:j1].bitcast(FP8X4),
+                scales=z_scales[b][:, j0:j1],
+                in_=z_bf[b][:, PACK * j0 : PACK * j1],
+            )
+
+        def second_pass(b, acc, j0):
+            for n in range(N // P):
+                nc.tensor.matmul_mx(
+                    out=acc[:, n, :],
+                    lhsT=w4_word_sb[:, b, 2 * P * n : 2 * P * (n + 1)].bitcast(FP4X4),
+                    lhsT_scale=w4_scale_sb[:, b, P * n : P * (n + 1)],
+                    rhs=z_codes[b][:, j0 : j0 + CHUNK].bitcast(FP8X4),
+                    rhs_scale=z_scales[b][:, j0 : j0 + CHUNK],
+                    start=(b == 0 and n == 0),
+                    stop=(b == 1 and n == N // P - 1),
+                )
+
+        slices = [(b, t) for b in range(2) for t in range(PACK)]
+        angles = [reduce_angle(*slices[0])]
+        piece = P // WEAVE_PIECES
+        for i, (b, t) in enumerate(slices):
+            if i + 1 < len(slices):
+                angles.append(reduce_angle(*slices[i + 1]))
+            h = make_h(b, t, *angles[i])
+            if i < 2:
+                for m0 in range(0, P, piece):
+                    weave_w(i, 1, "slot%d" % (4 + i), m0, m0 + piece, nc.vector.tensor_copy if m0 + P * i >= LATE_SHARE else nc.scalar.copy)
+                quantise_w(i, 1)
+            if i == 2:
+                w4_word_sb = keep.tile([P, 2, 2 * N], U8, name="w4_word_sb", tag="slot0", align_bytes=64)
+                nc.sync.dma_start(
+                    out=w4_word_sb[:].bitcast(I32), in_=w4_words.bitcast(I32).rearrange("a p c -> p a c")
+                )
+                w4_scale_sb = keep.tile([P, 2, N], U8, name="w4_scale_sb", tag="slot1", align_bytes=64)
+                nc.vector.memset(w4_scale_sb[:].rearrange("p a n -> p (a n)").bitcast(I32), 0)
+                for q in range(4):
+                    nc.sync.dma_start(
+                        out=w4_scale_sb[32 * q : 32 * q + 4, :, :].bitcast(I32),
+                        in_=w4_scales[:, 4 * q : 4 * q + 4, :].bitcast(I32).rearrange("a r c -> r a c"),
+                    )
+            if i + 1 < len(slices):
+                pick(b, t, h)
+            if i == PACK - 1:
+                join(0, 0, PAIRS)
+            if i == PACK:
+                quantise_z(0, 0, PAIRS)
+        pending = (b, t, h)
+        chunks = range(0, PAIRS, CHUNK)
+        accs = [psum.tile([P, N // P, CHUNK], F32, name="acc", tag="bank") for j0 in chunks]
+        for acc, j0 in zip(accs, chunks):
+            second_pass(0, acc, j0)
+        pick(*pending)
+        out_view = out.rearrange("(n p) j -> p n j", p=P)
+
+        def finish(q):
+            j0 = q * CHUNK
+            quantise_z(1, j0, j0 + CHUNK)
+            second_pass(1, accs[q], j0)
+            result = keep.tile([P, N // P, CHUNK], F32, name="result%d" % q)
+            nc.scalar.activation(result[:], accs[q][:], ACT.Tanh)
+            nc.sync.dma_start(out=out_view[:, :, j0 : j0 + CHUNK], in_=result[:])
+
+        for q, j0 in enumerate(chunks):
+            join(1, j0, j0 + CHUNK)
+            if q > 0:
+                finish(q - 1)
+        finish(len(chunks) - 1)

@@ -23,11 +23,10 @@ PASS = P * PACK
 BANK = 512
 TWO_PI = 2.0 * math.pi
 TURN_OFFSET = 1024.0
-VECTOR_TURN_SLICES = (0, 1, 2)
-TEST_OFFSET = 1.0
+VECTOR_TURN_HALVES = (0, 2, 4, 6)
 CHUNK = 128
 LATE_SHARE = 128
-SHIFT_BUFS = 2
+SHIFT_BUFS = 4
 H_BUFS = 3
 SCALAR_SHARE = 48
 WEAVE_PIECES = 4
@@ -49,9 +48,9 @@ def tile_list_slab_bookmatch_features_kernel(
         scale_table = keep.tile([P, T], U8, name="scale_table", tag="slot6", align_bytes=64)
         picked_scales = keep.tile([P, S], U8, name="picked_scales", align_bytes=64)
         v_scales = [keep.tile([P, S], U8, name="v_scales%d" % a, align_bytes=64) for a in range(2)]
-        nc.vector.memset(scale_table[0:96, :].bitcast(I32), 0)
+        nc.gpsimd.memset(scale_table[0:96, :].bitcast(I32), 0)
         for a in range(2):
-            nc.vector.memset(v_scales[a][:].bitcast(I32), 0)
+            nc.gpsimd.memset(v_scales[a][:].bitcast(I32), 0)
 
         w_raw = {}
 
@@ -165,28 +164,29 @@ def tile_list_slab_bookmatch_features_kernel(
                         stop=(a == 1),
                     )
                 sums.append((x, cols))
-            if PACK * b + t in VECTOR_TURN_SLICES:
-                turns = ring.tile([P, S], I32, name="turns_i", bufs=1)
-                for x, cols in sums:
-                    nc.vector.tensor_scalar(turns[:, cols], x[:], 1.0 / TWO_PI, TEST_OFFSET, ALU.mult, ALU.add)
-                for x, cols in sums:
-                    nc.vector.scalar_tensor_tensor(angle[:, cols], turns[:, cols], -TWO_PI, x[:], ALU.mult, ALU.add)
-                return angle, TEST_OFFSET * TWO_PI
-            turns = ring.tile([P, S], U32, name="turns_u", bufs=1)
-            shift = ring.tile([P, S], F32, name="shift", bufs=SHIFT_BUFS)
-            for x, cols in sums:
-                nc.scalar.activation(turns[:, cols], x[:], ACT.Copy, bias=TURN_OFFSET, scale=1.0 / TWO_PI)
-            for x, cols in sums:
-                nc.scalar.activation(shift[:, cols], turns[:, cols], ACT.Copy, bias=TURN_OFFSET * TWO_PI, scale=-TWO_PI)
-            for x, cols in sums:
-                nc.vector.tensor_tensor(angle[:, cols], x[:], shift[:, cols], ALU.add)
-            return angle, 0.0
+            on_vector = [2 * (PACK * b + t) + u in VECTOR_TURN_HALVES for u in range(2)]
+            turns = [None, None]
+            for u, (x, cols) in enumerate(sums):
+                if on_vector[u]:
+                    turns[u] = ring.tile([P, BANK], I32, name="turns_signed", bufs=2)
+                    nc.vector.tensor_scalar(turns[u][:], x[:], 1.0 / TWO_PI, None, ALU.mult)
+                else:
+                    turns[u] = ring.tile([P, BANK], U32, name="turns_offset", bufs=2)
+                    nc.scalar.activation(turns[u][:], x[:], ACT.Copy, bias=TURN_OFFSET, scale=1.0 / TWO_PI)
+            for u, (x, cols) in enumerate(sums):
+                if on_vector[u]:
+                    nc.vector.scalar_tensor_tensor(angle[:, cols], turns[u][:], -TWO_PI, x[:], ALU.mult, ALU.add)
+                else:
+                    shift = ring.tile([P, BANK], F32, name="shift", bufs=SHIFT_BUFS)
+                    nc.scalar.activation(shift[:], turns[u][:], ACT.Copy, bias=TURN_OFFSET * TWO_PI, scale=-TWO_PI)
+                    nc.vector.tensor_tensor(angle[:, cols], x[:], shift[:], ALU.add)
+            return angle
 
-        def make_h(b, t, angle, bias):
+        def make_h(b, t, angle):
             bands = ring.tile([P, S], F32, name="bands", bufs=1)
             h = ring.tile([P, S], F32, name="h", bufs=H_BUFS)
             for cols in halves:
-                nc.scalar.activation(bands[:, cols], angle[:, cols], ACT.Sin, bias=bias)
+                nc.scalar.activation(bands[:, cols], angle[:, cols], ACT.Sin)
             for cols in halves:
                 nc.scalar.activation(h[:, cols], bands[:, cols], ACT.Copy, scale=gain_sb[:, b, t : t + 1])
             return h
@@ -230,7 +230,7 @@ def tile_list_slab_bookmatch_features_kernel(
         for i, (b, t) in enumerate(slices):
             if i + 1 < len(slices):
                 angles.append(reduce_angle(*slices[i + 1]))
-            h = make_h(b, t, *angles[i])
+            h = make_h(b, t, angles[i])
             if i < 2:
                 for m0 in range(0, P, piece):
                     weave_w(i, 1, "slot%d" % (4 + i), m0, m0 + piece, nc.vector.tensor_copy if m0 + P * i >= LATE_SHARE else nc.scalar.copy)
@@ -241,7 +241,7 @@ def tile_list_slab_bookmatch_features_kernel(
                     out=w4_word_sb[:].bitcast(I32), in_=w4_words.bitcast(I32).rearrange("a p c -> p a c")
                 )
                 w4_scale_sb = keep.tile([P, 2, N], U8, name="w4_scale_sb", tag="slot1", align_bytes=64)
-                nc.vector.memset(w4_scale_sb[:].rearrange("p a n -> p (a n)").bitcast(I32), 0)
+                nc.gpsimd.memset(w4_scale_sb[:].rearrange("p a n -> p (a n)").bitcast(I32), 0)
                 for q in range(4):
                     nc.sync.dma_start(
                         out=w4_scale_sb[32 * q : 32 * q + 4, :, :].bitcast(I32),

@@ -23,8 +23,10 @@ PASS = P * PACK
 BANK = 512
 TWO_PI = 2.0 * math.pi
 TURN_OFFSET = 1024.0
-VECTOR_TURN_HALVES = (0, 2, 4, 6)
+VECTOR_TURN_HALVES = (0, 1, 2, 3)
 CHUNK = 128
+GPSIMD_SHARE = 128
+N_GROUP = 2
 LATE_SHARE = 128
 SHIFT_BUFS = 4
 H_BUFS = 3
@@ -110,6 +112,9 @@ def tile_list_slab_bookmatch_features_kernel(
                 in_=w_raw[a, b][:].rearrange("p i (m t) -> p m i t", t=PACK)[:, m0:m1],
             )
 
+        def gpsimd_copy(out, in_):
+            nc.gpsimd.tensor_scalar(out, in_, 1.0, 0.0, ALU.mult, ALU.add)
+
         def quantise_w(a, b):
             codes = keep.tile([P, PASS], U32, name="w_codes%d%d" % (a, b), align_bytes=64)
             scales = keep.tile([P, PASS], U8, name="w_scales%d%d" % (a, b), align_bytes=64)
@@ -135,8 +140,8 @@ def tile_list_slab_bookmatch_features_kernel(
             quantise_w(a, 0)
         pick_words(1)
         load_w(0, 1, "slot0")
-        load_polish(0, "slot2")
-        load_w(1, 1, "slot1")
+        load_w(1, 1, "slot2")
+        load_polish(0, "slot1")
         load_polish(1, "slot3")
 
         left = [keep.tile([P, PACK, PAIRS], F32, name="left%d" % b) for b in range(2)]
@@ -212,16 +217,17 @@ def tile_list_slab_bookmatch_features_kernel(
                 in_=z_bf[b][:, PACK * j0 : PACK * j1],
             )
 
-        def second_pass(b, acc, j0):
-            for n in range(N // P):
+        def second_pass(b, acc, n0, j0):
+            for e in range(N_GROUP):
+                n = n0 + e
                 nc.tensor.matmul_mx(
-                    out=acc[:, n, :],
+                    out=acc[:, e, :],
                     lhsT=w4_word_sb[:, b, 2 * P * n : 2 * P * (n + 1)].bitcast(FP4X4),
                     lhsT_scale=w4_scale_sb[:, b, P * n : P * (n + 1)],
                     rhs=z_codes[b][:, j0 : j0 + CHUNK].bitcast(FP8X4),
                     rhs_scale=z_scales[b][:, j0 : j0 + CHUNK],
-                    start=(b == 0 and n == 0),
-                    stop=(b == 1 and n == N // P - 1),
+                    start=(b == 0 and e == 0),
+                    stop=(b == 1 and e == N_GROUP - 1),
                 )
 
         slices = [(b, t) for b in range(2) for t in range(PACK)]
@@ -233,14 +239,14 @@ def tile_list_slab_bookmatch_features_kernel(
             h = make_h(b, t, angles[i])
             if i < 2:
                 for m0 in range(0, P, piece):
-                    weave_w(i, 1, "slot%d" % (4 + i), m0, m0 + piece, nc.vector.tensor_copy if m0 + P * i >= LATE_SHARE else nc.scalar.copy)
+                    weave_w(i, 1, "slot%d" % (4 + i), m0, m0 + piece, gpsimd_copy if m0 + P * i < GPSIMD_SHARE else nc.vector.tensor_copy if m0 + P * i >= LATE_SHARE else nc.scalar.copy)
                 quantise_w(i, 1)
             if i == 2:
                 w4_word_sb = keep.tile([P, 2, 2 * N], U8, name="w4_word_sb", tag="slot0", align_bytes=64)
                 nc.sync.dma_start(
                     out=w4_word_sb[:].bitcast(I32), in_=w4_words.bitcast(I32).rearrange("a p c -> p a c")
                 )
-                w4_scale_sb = keep.tile([P, 2, N], U8, name="w4_scale_sb", tag="slot1", align_bytes=64)
+                w4_scale_sb = keep.tile([P, 2, N], U8, name="w4_scale_sb", tag="slot2", align_bytes=64)
                 nc.gpsimd.memset(w4_scale_sb[:].rearrange("p a n -> p (a n)").bitcast(I32), 0)
                 for q in range(4):
                     nc.sync.dma_start(
@@ -255,19 +261,23 @@ def tile_list_slab_bookmatch_features_kernel(
                 quantise_z(0, 0, PAIRS)
         pending = (b, t, h)
         chunks = range(0, PAIRS, CHUNK)
-        accs = [psum.tile([P, N // P, CHUNK], F32, name="acc", tag="bank") for j0 in chunks]
-        for acc, j0 in zip(accs, chunks):
-            second_pass(0, acc, j0)
+        n_starts = range(0, N // P, N_GROUP)
+        accs = {}
+        for j0 in chunks:
+            for n0 in n_starts:
+                accs[j0, n0] = psum.tile([P, N_GROUP, CHUNK], F32, name="acc", tag="bank")
+                second_pass(0, accs[j0, n0], n0, j0)
         pick(*pending)
         out_view = out.rearrange("(n p) j -> p n j", p=P)
 
         def finish(q):
             j0 = q * CHUNK
             quantise_z(1, j0, j0 + CHUNK)
-            second_pass(1, accs[q], j0)
-            result = keep.tile([P, N // P, CHUNK], F32, name="result%d" % q)
-            nc.scalar.activation(result[:], accs[q][:], ACT.Tanh)
-            nc.sync.dma_start(out=out_view[:, :, j0 : j0 + CHUNK], in_=result[:])
+            for n0 in n_starts:
+                second_pass(1, accs[j0, n0], n0, j0)
+                result = keep.tile([P, N_GROUP, CHUNK], F32, name="result%d%d" % (q, n0))
+                nc.scalar.activation(result[:], accs[j0, n0][:], ACT.Tanh)
+                nc.sync.dma_start(out=out_view[:, n0 : n0 + N_GROUP, j0 : j0 + CHUNK], in_=result[:])
 
         for q, j0 in enumerate(chunks):
             join(1, j0, j0 + CHUNK)

import math
from contextlib import ExitStack

import concourse.mybir as mybir

K, T, S, H, PAIRS, N = 1024, 4096, 1024, 1024, 512, 512
FLOPS = 2 * K * H * S + 2 * H * N * PAIRS

F32 = mybir.dt.float32
BF16 = mybir.dt.bfloat16
I32 = mybir.dt.int32
U32 = mybir.dt.uint32
U16 = mybir.dt.uint16
U8 = mybir.dt.uint8
FP8X4 = mybir.dt.float8_e4m3fn_x4
FP4X4 = mybir.dt.float4_e2m1fn_x4
ALU = mybir.AluOpType
ACT = mybir.ActivationFunctionType

P = 128
PACK = 4
PASS = P * PACK
BANK = 512
TWO_PI = 2.0 * math.pi
TURN_OFFSET = 1024.0
VECTOR_TURN_HALVES = (0, 1, 2, 3)
CHUNK = 128
GPSIMD_SHARE = 128
N_GROUP = 2
LATE_SHARE = 128
SHIFT_BUFS = 4
H_BUFS = 3
SCALAR_SHARE = 48
WEAVE_PIECES = 4


def tile_list_slab_bookmatch_features_kernel(
    tc, tab_words, tab_scales, offs, w1, gain, pos1, pos2, polish, w4_words, w4_scales, out
):
    nc = tc.nc
    with ExitStack() as ctx:
        keep = ctx.enter_context(tc.tile_pool(name="keep", bufs=1))
        ring = ctx.enter_context(tc.tile_pool(name="ring", bufs=2))
        psum = ctx.enter_context(tc.psum_pool(name="psum", bufs=8))

        offs_sb = keep.tile([P, S // 16], U16, name="offs_sb")
        pos1_sb = keep.tile([P, PAIRS // 16], U16, name="pos1_sb")
        pos2_sb = keep.tile([P, PAIRS // 16], U16, name="pos2_sb")

        scale_table = keep.tile([P, T], U8, name="scale_table", tag="slot6", align_bytes=64)
        picked_scales = keep.tile([P, S], U8, name="picked_scales", align_bytes=64)
        v_scales = [keep.tile([P, S], U8, name="v_scales%d" % a, align_bytes=64) for a in range(2)]
        nc.gpsimd.memset(scale_table[0:96, :].bitcast(I32), 0)
        for a in range(2):
            nc.gpsimd.memset(v_scales[a][:].bitcast(I32), 0)

        w_raw = {}

        def load_w(a, b, tag):
            raw = keep.tile([P, PACK, PASS], F32, name="w_raw%d%d" % (a, b), tag=tag, align_bytes=64)
            rows = w1[a * PASS : (a + 1) * PASS, b * PASS : (b + 1) * PASS]
            nc.sync.dma_start(out=raw[:], in_=rows.rearrange("(p i) c -> p i c", i=PACK))
            w_raw[a, b] = raw

        word_table = {}

        def load_words(a, tag):
            table = keep.tile([P, T], U16, name="word_table%d" % a, tag=tag, align_bytes=64)
            nc.sync.dma_start(out=table[:].bitcast(I32), in_=tab_words[a].bitcast(I32))
            word_table[a] = table

        def move_scales(a):
            for q in range(4):
                row = 96 + 16 * a + 4 * q
                nc.sync.dma_start(
                    out=v_scales[a][32 * q : 32 * q + 4, :].bitcast(I32),
                    in_=picked_scales[row : row + 4, :].bitcast(I32),
                )

        polish_sb = {}

        def load_polish(b, tag):
            pol = keep.tile([P, PACK, PAIRS], F32, name="polish%d" % b, tag=tag, align_bytes=64)
            rows = polish[b * PASS : (b + 1) * PASS, :].rearrange("(p t) j -> p t j", t=PACK)
            nc.sync.dma_start(out=pol[:], in_=rows)
            polish_sb[b] = pol

        nc.sync.dma_start(
            out=scale_table[96:128, :].bitcast(I32),
            in_=tab_scales.rearrange("a q t -> (a q) t").bitcast(I32),
        )
        nc.sync.dma_start(offs_sb[:], offs)
        load_words(0, "slot7")
        nc.sync.dma_start(pos1_sb[:], pos1)
        nc.sync.dma_start(pos2_sb[:], pos2)
        gain_sb = keep.tile([P, 2, PACK], F32, name="gain_sb")
        nc.sync.dma_start(out=gain_sb[:], in_=gain.rearrange("(b p t) -> p b t", b=2, t=PACK))
        load_w(0, 0, "slot0")
        load_w(1, 0, "slot1")

        w_codes, w_scales = {}, {}

        w_grouped = {}

        def weave_w(a, b, tag, m0, m1, engine_copy):
            if (a, b) not in w_grouped:
                w_grouped[a, b] = keep.tile(
                    [P, PACK * PASS], BF16, name="w_grouped%d%d" % (a, b), tag=tag, align_bytes=64
                )
            engine_copy(
                out=w_grouped[a, b][:].rearrange("p (t m i) -> p m i t", t=PACK, i=PACK)[:, m0:m1],
                in_=w_raw[a, b][:].rearrange("p i (m t) -> p m i t", t=PACK)[:, m0:m1],
            )

        def gpsimd_copy(out, in_):
            nc.gpsimd.tensor_scalar(out, in_, 1.0, 0.0, ALU.mult, ALU.add)

        def quantise_w(a, b):
            codes = keep.tile([P, PASS], U32, name="w_codes%d%d" % (a, b), align_bytes=64)
            scales = keep.tile([P, PASS], U8, name="w_scales%d%d" % (a, b), align_bytes=64)
            nc.vector.quantize_mx(out=codes[:].bitcast(FP8X4), scales=scales[:], in_=w_grouped[a, b][:])
            w_codes[a, b], w_scales[a, b] = codes, scales

        v_words = {}

        def pick_words(a):
            for u in range(2):
                words = keep.tile([P, BANK], U16, name="v_words%d%d" % (a, u), align_bytes=64)
                nc.vector.tensor_copy(words[:], word_table[a][:].indirect(offs_sb[:, 32 * u : 32 * u + 32]))
                v_words[a, u] = words

        nc.vector.tensor_copy(picked_scales[:], scale_table[:].indirect(offs_sb[:]))
        move_scales(0)
        load_words(1, "slot6")
        move_scales(1)
        pick_words(0)
        for a in range(2):
            weave_w(a, 0, "slot%d" % (2 + a), 0, SCALAR_SHARE, nc.scalar.copy)
            weave_w(a, 0, "slot%d" % (2 + a), SCALAR_SHARE, P, nc.vector.tensor_copy)
            quantise_w(a, 0)
        pick_words(1)
        load_w(0, 1, "slot0")
        load_w(1, 1, "slot2")
        load_polish(0, "slot1")
        load_polish(1, "slot3")

        left = [keep.tile([P, PACK, PAIRS], F32, name="left%d" % b) for b in range(2)]
        right = [keep.tile([P, PACK, PAIRS], F32, name="right%d" % b) for b in range(2)]
        z_codes = [keep.tile([P, PAIRS], U32, name="z_codes%d" % b, align_bytes=64) for b in range(2)]
        z_scales = [keep.tile([P, PAIRS], U8, name="z_scales%d" % b, align_bytes=64) for b in range(2)]
        z_bf = [keep.tile([P, PACK * PAIRS], BF16, name="z_bf%d" % b, align_bytes=64) for b in range(2)]

        halves = [slice(u * BANK, (u + 1) * BANK) for u in range(2)]

        def reduce_angle(b, t):
            m_cols = slice(t * P, (t + 1) * P)
            angle = ring.tile([P, S], F32, name="angle")
            sums = []
            for u, cols in enumerate(halves):
                x = psum.tile([P, BANK], F32, name="x", tag="bank")
                for a in range(2):
                    nc.tensor.matmul_mx(
                        out=x[:],
                        lhsT=w_codes[a, b][:, m_cols].bitcast(FP8X4),
                        lhsT_scale=w_scales[a, b][:, m_cols],
                        rhs=v_words[a, u][:].bitcast(FP4X4),
                        rhs_scale=v_scales[a][:, cols],
                        start=(a == 0),
                        stop=(a == 1),
                    )
                sums.append((x, cols))
            on_vector = [2 * (PACK * b + t) + u in VECTOR_TURN_HALVES for u in range(2)]
            turns = [None, None]
            for u, (x, cols) in enumerate(sums):
                if on_vector[u]:
                    turns[u] = ring.tile([P, BANK], I32, name="turns_signed", bufs=2)
                    nc.vector.tensor_scalar(turns[u][:], x[:], 1.0 / TWO_PI, None, ALU.mult)
                else:
                    turns[u] = ring.tile([P, BANK], U32, name="turns_offset", bufs=2)
                    nc.scalar.activation(turns[u][:], x[:], ACT.Copy, bias=TURN_OFFSET, scale=1.0 / TWO_PI)
            for u, (x, cols) in enumerate(sums):
                if on_vector[u]:
                    nc.vector.scalar_tensor_tensor(angle[:, cols], turns[u][:], -TWO_PI, x[:], ALU.mult, ALU.add)
                else:
                    shift = ring.tile([P, BANK], F32, name="shift", bufs=SHIFT_BUFS)
                    nc.scalar.activation(shift[:], turns[u][:], ACT.Copy, bias=TURN_OFFSET * TWO_PI, scale=-TWO_PI)
                    nc.vector.tensor_tensor(angle[:, cols], x[:], shift[:], ALU.add)
            return angle

        def make_h(b, t, angle):
            bands = ring.tile([P, S], F32, name="bands", bufs=1)
            h = ring.tile([P, S], F32, name="h", bufs=H_BUFS)
            for cols in halves:
                nc.scalar.activation(bands[:, cols], angle[:, cols], ACT.Sin)
            for cols in halves:
                nc.scalar.activation(h[:, cols], bands[:, cols], ACT.Copy, scale=gain_sb[:, b, t : t + 1])
            return h

        def pick(b, t, h):
            nc.vector.tensor_tensor(
                left[b][:, t, :], h[:].indirect(pos1_sb[:]), polish_sb[b][:, t, :], ALU.add
            )
            nc.vector.tensor_copy(right[b][:, t, :], h[:].indirect(pos2_sb[:]))

        def join(b, j0, j1):
            nc.vector.tensor_tensor(
                z_bf[b][:, PACK * j0 : PACK * j1].rearrange("p (c i t) -> p c t i", i=4, t=PACK),
                left[b][:, :, j0:j1].rearrange("p t (c i) -> p c t i", i=4),
                right[b][:, :, j0:j1].rearrange("p t (c i) -> p c t i", i=4),
                ALU.max,
            )

        def quantise_z(b, j0, j1):
            nc.vector.quantize_mx(
                out=z_codes[b][:, j0:j1].bitcast(FP8X4),
                scales=z_scales[b][:, j0:j1],
                in_=z_bf[b][:, PACK * j0 : PACK * j1],
            )

        def second_pass(b, acc, n0, j0):
            for e in range(N_GROUP):
                n = n0 + e
                nc.tensor.matmul_mx(
                    out=acc[:, e, :],
                    lhsT=w4_word_sb[:, b, 2 * P * n : 2 * P * (n + 1)].bitcast(FP4X4),
                    lhsT_scale=w4_scale_sb[:, b, P * n : P * (n + 1)],
                    rhs=z_codes[b][:, j0 : j0 + CHUNK].bitcast(FP8X4),
                    rhs_scale=z_scales[b][:, j0 : j0 + CHUNK],
                    start=(b == 0 and e == 0),
                    stop=(b == 1 and e == N_GROUP - 1),
                )

        slices = [(b, t) for b in range(2) for t in range(PACK)]
        angles = [reduce_angle(*slices[0])]
        piece = P // WEAVE_PIECES
        for i, (b, t) in enumerate(slices):
            if i + 1 < len(slices):
                angles.append(reduce_angle(*slices[i + 1]))
            h = make_h(b, t, angles[i])
            if i < 2:
                for m0 in range(0, P, piece):
                    weave_w(i, 1, "slot%d" % (4 + i), m0, m0 + piece, gpsimd_copy if m0 + P * i < GPSIMD_SHARE else nc.vector.tensor_copy if m0 + P * i >= LATE_SHARE else nc.scalar.copy)
                quantise_w(i, 1)
            if i == 2:
                w4_word_sb = keep.tile([P, 2, 2 * N], U8, name="w4_word_sb", tag="slot0", align_bytes=64)
                nc.sync.dma_start(
                    out=w4_word_sb[:].bitcast(I32), in_=w4_words.bitcast(I32).rearrange("a p c -> p a c")
                )
                w4_scale_sb = keep.tile([P, 2, N], U8, name="w4_scale_sb", tag="slot2", align_bytes=64)
                nc.gpsimd.memset(w4_scale_sb[:].rearrange("p a n -> p (a n)").bitcast(I32), 0)
                for q in range(4):
                    nc.sync.dma_start(
                        out=w4_scale_sb[32 * q : 32 * q + 4, :, :].bitcast(I32),
                        in_=w4_scales[:, 4 * q : 4 * q + 4, :].bitcast(I32).rearrange("a r c -> r a c"),
                    )
            if i + 1 < len(slices):
                pick(b, t, h)
            if i == PACK - 1:
                join(0, 0, PAIRS)
            if i == PACK:
                quantise_z(0, 0, PAIRS)
        pending = (b, t, h)
        chunks = range(0, PAIRS, CHUNK)
        n_starts = range(0, N // P, N_GROUP)
        accs = {}
        for j0 in chunks:
            for n0 in n_starts:
                accs[j0, n0] = psum.tile([P, N_GROUP, CHUNK], F32, name="acc", tag="bank")
                second_pass(0, accs[j0, n0], n0, j0)
        pick(*pending)
        out_view = out.rearrange("(n p) j -> p n j", p=P)

        def finish(q):
            j0 = q * CHUNK
            quantise_z(1, j0, j0 + CHUNK)
            for n0 in n_starts:
                second_pass(1, accs[j0, n0], n0, j0)
                result = keep.tile([P, N_GROUP, CHUNK], F32, name="result%d%d" % (q, n0))
                nc.scalar.activation(result[:], accs[j0, n0][:], ACT.Tanh)
                nc.sync.dma_start(out=out_view[:, n0 : n0 + N_GROUP, j0 : j0 + CHUNK], in_=result[:])

        for q, j0 in enumerate(chunks):
            join(1, j0, j0 + CHUNK)
            if q > 0:
                finish(q - 1)
        finish(len(chunks) - 1)
